import numpy as np
import ml_dtypes


def mxq(x, axis, fmt="e4m3"):
    dtype, down = {"e4m3": (ml_dtypes.float8_e4m3fn, 7), "e5m2": (ml_dtypes.float8_e5m2, 14)}[fmt]
    v = np.moveaxis(np.asarray(x, np.float32).astype(ml_dtypes.bfloat16).astype(np.float64), axis, -1)
    blocks = v.reshape(v.shape[:-1] + (-1, 32))
    amax = np.abs(blocks).max(-1, keepdims=True)
    byte = np.maximum(np.where(amax > 0, np.frexp(amax)[1] - 1 + 127, 0) - down, 1)
    scale = np.exp2(byte - 127.0)
    codes = (blocks / scale).astype(np.float32).astype(dtype).astype(np.float64)
    return np.moveaxis((codes * scale).reshape(v.shape), -1, axis)


WIDE = False


def mx_kscale(k):
    if not WIDE:
        return np.ones(k)
    levels = np.array([10, -10, 5, -5, 0])
    if k % 512:
        return np.exp2(np.random.permutation(np.resize(levels, k // 32))).repeat(32)
    a = np.empty((k // 512, 16))
    for p in range(k // 512):
        a[p, :8] = np.random.permutation(np.resize(levels, 8))
        for g in range(8):
            far = levels[np.abs(levels - a[p, g]) >= 10]
            a[p, g + 8] = far[np.random.randint(len(far))]
    return np.exp2(a.ravel()).repeat(32)


def f64(x):
    return np.asarray(x).astype(np.float64)


def striped(idx):
    return np.tile(np.asarray(idx).reshape(-1, 16).T, (8, 1)).astype(np.uint16)


def unstriped(offs):
    return offs[:16].T.reshape(-1).astype(np.int64)


E2M1 = np.array([0.0, 0.5, 1.0, 1.5, 2.0, 3.0, 4.0, 6.0, -0.0, -0.5, -1.0, -1.5, -2.0, -3.0, -4.0, -6.0])


def pack_weight(w, fmt):
    k, n = w.shape
    w = f64(np.asarray(w, np.float32).astype(ml_dtypes.bfloat16)).reshape(k // 32, 32, n)
    amax = np.abs(w).max(1)
    if fmt == "e4m3":
        byte = np.frexp(amax)[1] - 1 + 127 - 7
    else:
        mant, ex = np.frexp(amax / 6.0)
        byte = np.where(mant > 0.5, ex, ex - 1) + 127
    byte = np.clip(np.where(amax > 0, byte, 1), 1, 254)
    scaled = (w * np.exp2(127.0 - byte)[:, None, :]).reshape(k, n).astype(np.float32)
    by_word = np.ascontiguousarray(scaled.reshape(k // 512, 128, 4, n).transpose(0, 1, 3, 2))
    if fmt == "e4m3":
        words = by_word.astype(ml_dtypes.float8_e4m3fn).view(np.uint8)
    else:
        c = by_word.astype(ml_dtypes.float4_e2m1fn).view(np.uint8) & 0xF
        words = (c[..., 0::2] | (c[..., 1::2] << 4)).reshape(k // 512, 128, 2 * n)
    return np.ascontiguousarray(words), np.ascontiguousarray(byte.astype(np.uint8).reshape(k // 512, 16, n))


def unpack_weight(words, scales, fmt):
    g, _, n = scales.shape
    words = np.ascontiguousarray(words).reshape(g, 128, n, -1)
    if fmt == "e4m3":
        vals = words.view(ml_dtypes.float8_e4m3fn).astype(np.float64)
    else:
        nib = np.empty((g, 128, n, 4), np.uint8)
        nib[..., 0::2] = words & 0xF
        nib[..., 1::2] = words >> 4
        vals = E2M1[nib]
    vals = vals * np.repeat(np.exp2(scales.astype(np.float64) - 127.0), 8, axis=1)[..., None]
    return vals.transpose(0, 1, 3, 2).reshape(g * 512, n)


def sigmoid(v):
    return 1.0 / (1.0 + np.exp(-v))


D, T, I, Q, G, E = 512, 2048, 512, 256, 32, 512


def setup_inputs():
    n = np.random.standard_normal
    idx = np.random.permutation(T)[:I]
    fd = mx_kscale(D)
    fi = mx_kscale(I)
    ti = np.ones(T)
    ti[idx] = fi
    keysp = pack_weight(n((D, T)) / fd[:, None], "e4m3")
    return {
        "query": (n((D, Q)) * 1.0 / np.sqrt(D) * fd[:, None]).astype(np.float32),
        "keys_words": keysp[0],
        "keys_scales": keysp[1],
        "steep": (np.random.uniform(1.0, 4.0, (I, 1))).astype(np.float32),
        "us": (np.random.uniform(0.02, 0.1, (I, 1)) * fi[:, None]).astype(np.float32),
        "vals": (n((E, T)) / ti).astype(np.float32),
        "offs": striped(idx),
    }


def reference(query, keys_words, keys_scales, steep, us, vals, offs):
    idx = unstriped(offs)
    keysu = unpack_weight(keys_words, keys_scales, "e4m3")
    keysidxg = keysu[:, idx]
    queryq = mxq(f64(query), 0, "e4m3")
    a = keysidxg.T @ queryq
    b = a.reshape(I, G, Q // G).mean(axis=2)
    br = np.repeat(b, Q // G, axis=1)
    w = sigmoid((a - br) * f64(steep)) * f64(us)
    vt = f64(vals)[:, idx].T
    wq = mxq(w, 0, "e4m3")
    vtq = mxq(vt, 0, "e4m3")
    o = wq.T @ vtq
    return o

@@ -1,0 +1,207 @@
+from contextlib import ExitStack
+
+import concourse.mybir as mybir
+from concourse.masks import make_identity
+
+D, T, I, Q, E = 512, 2048, 512, 256, 512
+TEAM = 8
+FLOPS = 2 * D * I * Q + 2 * I * Q * E
+
+F32 = mybir.dt.float32
+BF16 = mybir.dt.bfloat16
+I32 = mybir.dt.int32
+U32 = mybir.dt.uint32
+U16 = mybir.dt.uint16
+U8 = mybir.dt.uint8
+FP8X4 = mybir.dt.float8_e4m3fn_x4
+ACT = mybir.ActivationFunctionType
+ALU = mybir.AluOpType
+AXIS = mybir.AxisListType
+
+P = 128
+PACK = 4
+E_BLOCKS = E // P
+Q_HALVES = Q // P
+
+
+def tile_attend_teamcontrast_kernel(tc, query, keys_words, keys_scales, steep, us, vals, offs, out):
+    nc = tc.nc
+    with ExitStack() as ctx:
+        keep = ctx.enter_context(tc.tile_pool(name="keep", bufs=1))
+        score_ps = ctx.enter_context(tc.psum_pool(name="score_ps", bufs=1))
+        turn_ps = ctx.enter_context(tc.psum_pool(name="turn_ps", bufs=2))
+        out_ps = ctx.enter_context(tc.psum_pool(name="out_ps", bufs=1))
+
+        offsets = keep.tile([P, I // 16], U16, name="offsets")
+        nc.sync.dma_start(offsets[:], offs)
+
+        key_scale_pool = keep.tile([P, T], U8, name="key_scale_pool", tag="kscale", align_bytes=64)
+        nc.gpsimd.memset(key_scale_pool[:].bitcast(I32), 0)
+        q_raw = keep.tile([P, PACK, Q], F32, name="q_raw")
+        nc.sync.dma_start(q_raw[:], query.rearrange("(p j) q -> p j q", j=PACK))
+        for quad in range(4):
+            nc.sync.dma_start(
+                key_scale_pool[32 * quad : 32 * quad + 4, :].bitcast(I32),
+                keys_scales[0, 4 * quad : 4 * quad + 4, :].bitcast(I32),
+            )
+        key_word_pool = keep.tile([P, T], I32, name="key_word_pool", align_bytes=64)
+        nc.sync.dma_start(key_word_pool[:], keys_words[0].rearrange("p n t -> p (n t)").bitcast(I32))
+        steep_sb = keep.tile([P, PACK], F32, name="steep_sb")
+        nc.sync.dma_start(steep_sb[:], steep.rearrange("(p r) o -> p (r o)", r=PACK))
+        us_sb = keep.tile([P, PACK], F32, name="us_sb")
+        nc.sync.dma_start(us_sb[:], us.rearrange("(p r) o -> p (r o)", r=PACK))
+        val_pool = []
+        for b in range(E_BLOCKS):
+            t = keep.tile([P, T], F32, name="val_pool%d" % b, tag="val%d" % b, align_bytes=64)
+            nc.sync.dma_start(t[:], vals[b * P : (b + 1) * P, :])
+            val_pool.append(t)
+
+        ident = keep.tile([P, P], F32, name="ident")
+        make_identity(nc, ident[:])
+
+        warm = keep.tile([P, 1], F32, name="warm")
+        nc.vector.memset(warm[:], 0.0)
+        warmed = keep.tile([P, 1], F32, name="warmed")
+        nc.scalar.activation(warmed[:], warm[:], ACT.Sigmoid)
+        q_bf = keep.tile([P, Q, PACK], BF16, name="q_bf", align_bytes=64)
+        nc.scalar.copy(
+            q_bf[:].rearrange("p (c i) t -> p c t i", i=4),
+            q_raw[:].rearrange("p t (c i) -> p c t i", i=4),
+        )
+        ks_list = keep.tile([P, I], U8, name="ks_list", align_bytes=64)
+        nc.vector.tensor_copy(ks_list[:], key_scale_pool[:].indirect(offsets[:]))
+        k_scales = keep.tile([P, PACK, P], U8, name="k_scales", align_bytes=64)
+        nc.vector.tensor_copy(k_scales[:], ks_list[:].rearrange("p (s r) -> p r s", r=PACK))
+        q_codes = keep.tile([P, Q], U32, name="q_codes", tag="kscale", align_bytes=64)
+        q_scales = keep.tile([P, Q], U8, name="q_scales", align_bytes=64)
+        nc.vector.quantize_mx(
+            out=q_codes[:].bitcast(FP8X4), scales=q_scales[:], in_=q_bf[:].rearrange("p q t -> p (q t)")
+        )
+        k_codes = keep.tile([P, PACK, P], U32, name="k_codes", align_bytes=64)
+        nc.vector.tensor_copy(
+            k_codes[:].rearrange("p r s -> p s r"), key_word_pool[:].bitcast(U32).indirect(offsets[:])
+        )
+
+        scores = []
+        for pair in range(2):
+            bank = score_ps.tile([P, 2, Q], F32, name="scores%d" % pair)
+            for e in range(2):
+                r = 2 * pair + e
+                nc.tensor.matmul_mx(
+                    out=bank[:, e, :],
+                    lhsT=k_codes[:, r, :].bitcast(FP8X4),
+                    lhsT_scale=k_scales[:, r, :],
+                    rhs=q_codes[:].bitcast(FP8X4),
+                    rhs_scale=q_scales[:],
+                    start=True,
+                    stop=True,
+                )
+            scores.append(bank)
+
+        teams = 2 * Q // TEAM
+        sums, diffs = [], []
+        for pair in range(2):
+            s = keep.tile([P, teams], F32, name="team_sum%d" % pair, tag="slot%d" % pair, align_bytes=64)
+            nc.vector.tensor_reduce(
+                s[:], scores[pair][:].rearrange("p e (g j) -> p (e g) j", j=TEAM), AXIS.X, ALU.add
+            )
+            sums.append(s)
+        for pair in range(2):
+            d = keep.tile([P, teams, TEAM], F32, name="diff%d" % pair, align_bytes=64)
+            nc.vector.scalar_tensor_tensor(
+                d[:],
+                sums[pair][:].unsqueeze(2).to_broadcast([P, teams, TEAM]),
+                -1.0 / TEAM,
+                scores[pair][:].rearrange("p e (g j) -> p (e g) j", j=TEAM),
+                ALU.mult,
+                ALU.add,
+            )
+            diffs.append(d)
+
+        w_planes = keep.tile([P, PACK, Q], BF16, name="w_planes", align_bytes=64)
+        gates = []
+        for r in range(PACK):
+            g = keep.tile([P, Q], F32, name="gate%d" % r)
+            d = diffs[r // 2][:].rearrange("p (e g) j -> p e (g j)", e=2)
+            nc.scalar.activation(g[:], d[:, r % 2, :], ACT.Sigmoid, scale=steep_sb[:, r : r + 1])
+            gates.append(g)
+        for r in range(PACK):
+            nc.scalar.activation(w_planes[:, r, :], gates[r][:], ACT.Copy, scale=us_sb[:, r : r + 1])
+
+        early_bf = keep.tile([P, Q + 2 * P, PACK], BF16, name="early_bf", align_bytes=64)
+        nc.scalar.copy(
+            early_bf[:, 0:Q, :].rearrange("p (c i) t -> p c t i", i=4),
+            w_planes[:].rearrange("p t (c i) -> p c t i", i=4),
+        )
+
+        picked = {}
+
+        def gather(b):
+            g = keep.tile([P, I], BF16, name="picked%d" % b, tag="slot%d" % b, align_bytes=64)
+            nc.vector.tensor_copy(g[:], val_pool[b][:].indirect(offsets[:]))
+            picked[b] = g
+
+        def turn(b, v_bf):
+            words = picked[b][:].bitcast(F32)
+            xt = turn_ps.tile([P, 2, P], F32, name="xt")
+            for u in range(2):
+                nc.tensor.transpose(xt[:, u, :], words[:, u : I // 2 : 2], ident[:])
+            nc.scalar.copy(v_bf.bitcast(F32), xt[:].rearrange("p u e -> p e u"))
+
+        out_v = out.rearrange("(h p) e -> p h e", p=P)
+
+        def quantise(name, tag, v_bf, width):
+            v_codes = keep.tile([P, width], U32, name="codes" + name, tag=tag, align_bytes=64)
+            v_scales = keep.tile([P, width], U8, name="scales" + name, align_bytes=64)
+            nc.vector.quantize_mx(
+                out=v_codes[:].bitcast(FP8X4), scales=v_scales[:], in_=v_bf[:].rearrange("p e t -> p (e t)")
+            )
+            return v_codes, v_scales
+
+        def multiply(acc, h, operand):
+            nc.tensor.matmul_mx(
+                out=acc,
+                lhsT=early_codes[:, h * P : (h + 1) * P].bitcast(FP8X4),
+                lhsT_scale=early_scales[:, h * P : (h + 1) * P],
+                rhs=operand[0].bitcast(FP8X4),
+                rhs_scale=operand[1],
+                start=True,
+                stop=True,
+            )
+
+        v2 = keep.tile([P, P, PACK], BF16, name="v2", align_bytes=64)
+        v3 = keep.tile([P, P, PACK], BF16, name="v3", align_bytes=64)
+        gather(0)
+        turn(0, early_bf[:, Q : Q + P, :])
+        gather(1)
+        turn(1, early_bf[:, Q + P : Q + 2 * P, :])
+        gather(2)
+        turn(2, v2[:])
+        early_codes, early_scales = quantise("_early", "val2", early_bf, Q + 2 * P)
+        op01 = (early_codes[:, Q : Q + 2 * P], early_scales[:, Q : Q + 2 * P])
+        acc01 = out_ps.tile([P, Q_HALVES, 2 * P], F32, name="acc01")
+        for h in range(Q_HALVES):
+            multiply(acc01[:, h, :], h, op01)
+        res01 = keep.tile([P, Q_HALVES, 2 * P], F32, name="res01")
+        nc.scalar.copy(res01[:], acc01[:])
+        nc.sync.dma_start(out_v[:, :, 0 : 2 * P], res01[:])
+        gather(3)
+        turn(3, v3[:])
+        op2 = [t[:] for t in quantise("2", "val3", v2, P)]
+        acc2 = out_ps.tile([P, Q_HALVES, P], F32, name="acc2")
+        for h in range(Q_HALVES):
+            multiply(acc2[:, h, :], h, op2)
+        res2 = keep.tile([P, Q_HALVES, P], F32, name="res2")
+        nc.vector.tensor_copy(res2[:], acc2[:])
+        nc.sync.dma_start(out_v[:, :, 2 * P : 3 * P], res2[:])
+        op3 = [t[:] for t in quantise("3", "codes3", v3, P)]
+        for h in range(Q_HALVES):
+            acc3 = out_ps.tile([P, P], F32, name="acc3_%d" % h)
+            multiply(acc3[:], h, op3)
+            res3 = keep.tile([P, P], F32, name="res3_%d" % h)
+            if h == 0:
+                nc.scalar.copy(res3[:], acc3[:])
+                nc.scalar.dma_start(out_v[:, h, 3 * P : E], res3[:])
+            else:
+                nc.vector.tensor_copy(res3[:], acc3[:])
+                nc.sync.dma_start(out_v[:, h, 3 * P : E], res3[:])

@@ -29,8 +29,7 @@ def tile_attend_teamcontrast_kernel(tc, query, keys_words, keys_scales, steep, u
     with ExitStack() as ctx:
         keep = ctx.enter_context(tc.tile_pool(name="keep", bufs=1))
         score_ps = ctx.enter_context(tc.psum_pool(name="score_ps", bufs=1))
-        turn_ps = ctx.enter_context(tc.psum_pool(name="turn_ps", bufs=2))
-        out_ps = ctx.enter_context(tc.psum_pool(name="out_ps", bufs=1))
+        turn_ps = ctx.enter_context(tc.psum_pool(name="turn_ps", bufs=4))
 
         offsets = keep.tile([P, I // 16], U16, name="offsets")
         nc.sync.dma_start(offsets[:], offs)
@@ -82,50 +81,58 @@ def tile_attend_teamcontrast_kernel(tc, query, keys_words, keys_scales, steep, u
             k_codes[:].rearrange("p r s -> p s r"), key_word_pool[:].bitcast(U32).indirect(offsets[:])
         )
 
-        scores = []
-        for pair in range(2):
-            bank = score_ps.tile([P, 2, Q], F32, name="scores%d" % pair)
-            for e in range(2):
-                r = 2 * pair + e
-                nc.tensor.matmul_mx(
-                    out=bank[:, e, :],
-                    lhsT=k_codes[:, r, :].bitcast(FP8X4),
-                    lhsT_scale=k_scales[:, r, :],
-                    rhs=q_codes[:].bitcast(FP8X4),
-                    rhs_scale=q_scales[:],
-                    start=True,
-                    stop=True,
-                )
-            scores.append(bank)
-
-        teams = 2 * Q // TEAM
-        sums, diffs = [], []
-        for pair in range(2):
-            s = keep.tile([P, teams], F32, name="team_sum%d" % pair, tag="slot%d" % pair, align_bytes=64)
-            nc.vector.tensor_reduce(
-                s[:], scores[pair][:].rearrange("p e (g j) -> p (e g) j", j=TEAM), AXIS.X, ALU.add
+        teams = Q // TEAM
+        scores, sums, diffs = [], [], []
+        for r in range(PACK):
+            bank = score_ps.tile([P, Q], F32, name="scores%d" % r, tag="bank%d" % r)
+            nc.tensor.matmul_mx(
+                out=bank[:],
+                lhsT=k_codes[:, r, :].bitcast(FP8X4),
+                lhsT_scale=k_scales[:, r, :],
+                rhs=q_codes[:].bitcast(FP8X4),
+                rhs_scale=q_scales[:],
+                start=True,
+                stop=True,
             )
+            scores.append(bank[:].rearrange("p (g j) -> p g j", j=TEAM))
+
+        def team_sum(r):
+            s = keep.tile([P, teams], F32, name="team_sum%d" % r, tag="slot%d" % ((r + 2) % 4), align_bytes=64)
+            nc.vector.tensor_reduce(s[:], scores[r], AXIS.X, ALU.add)
             sums.append(s)
-        for pair in range(2):
-            d = keep.tile([P, teams, TEAM], F32, name="diff%d" % pair, align_bytes=64)
+
+        def contrast(r):
+            d = keep.tile([P, teams, TEAM], F32, name="diff%d" % r, align_bytes=64)
             nc.vector.scalar_tensor_tensor(
                 d[:],
-                sums[pair][:].unsqueeze(2).to_broadcast([P, teams, TEAM]),
+                sums[r][:].unsqueeze(2).to_broadcast([P, teams, TEAM]),
                 -1.0 / TEAM,
-                scores[pair][:].rearrange("p e (g j) -> p (e g) j", j=TEAM),
+                scores[r],
                 ALU.mult,
                 ALU.add,
             )
             diffs.append(d)
 
+        team_sum(0)
+        for r in range(PACK):
+            if r + 1 < PACK:
+                team_sum(r + 1)
+            contrast(r)
+
         w_planes = keep.tile([P, PACK, Q], BF16, name="w_planes", align_bytes=64)
         gates = []
-        for r in range(PACK):
+
+        def gate(r):
             g = keep.tile([P, Q], F32, name="gate%d" % r)
-            d = diffs[r // 2][:].rearrange("p (e g) j -> p e (g j)", e=2)
-            nc.scalar.activation(g[:], d[:, r % 2, :], ACT.Sigmoid, scale=steep_sb[:, r : r + 1])
+            nc.scalar.activation(
+                g[:], diffs[r][:].rearrange("p g j -> p (g j)"), ACT.Sigmoid, scale=steep_sb[:, r : r + 1]
+            )
             gates.append(g)
+
+        gate(0)
         for r in range(PACK):
+            if r + 1 < PACK:
+                gate(r + 1)
             nc.scalar.activation(w_planes[:, r, :], gates[r][:], ACT.Copy, scale=us_sb[:, r : r + 1])
 
         early_bf = keep.tile([P, Q + 2 * P, PACK], BF16, name="early_bf", align_bytes=64)
@@ -179,7 +186,7 @@ def tile_attend_teamcontrast_kernel(tc, query, keys_words, keys_scales, steep, u
         turn(2, v2[:])
         early_codes, early_scales = quantise("_early", "val2", early_bf, Q + 2 * P)
         op01 = (early_codes[:, Q : Q + 2 * P], early_scales[:, Q : Q + 2 * P])
-        acc01 = out_ps.tile([P, Q_HALVES, 2 * P], F32, name="acc01")
+        acc01 = score_ps.tile([P, Q_HALVES, 2 * P], F32, name="acc01", tag="bank0")
         for h in range(Q_HALVES):
             multiply(acc01[:, h, :], h, op01)
         res01 = keep.tile([P, Q_HALVES, 2 * P], F32, name="res01")
@@ -188,7 +195,7 @@ def tile_attend_teamcontrast_kernel(tc, query, keys_words, keys_scales, steep, u
         gather(3)
         turn(3, v3[:])
         op2 = [t[:] for t in quantise("2", "val3", v2, P)]
-        acc2 = out_ps.tile([P, Q_HALVES, P], F32, name="acc2")
+        acc2 = score_ps.tile([P, Q_HALVES, P], F32, name="acc2", tag="bank1")
         for h in range(Q_HALVES):
             multiply(acc2[:, h, :], h, op2)
         res2 = keep.tile([P, Q_HALVES, P], F32, name="res2")
@@ -196,7 +203,7 @@ def tile_attend_teamcontrast_kernel(tc, query, keys_words, keys_scales, steep, u
         nc.sync.dma_start(out_v[:, :, 2 * P : 3 * P], res2[:])
         op3 = [t[:] for t in quantise("3", "codes3", v3, P)]
         for h in range(Q_HALVES):
-            acc3 = out_ps.tile([P, P], F32, name="acc3_%d" % h)
+            acc3 = score_ps.tile([P, P], F32, name="acc3_%d" % h, tag="bank%d" % (2 + h))
             multiply(acc3[:], h, op3)
             res3 = keep.tile([P, P], F32, name="res3_%d" % h)
             if h == 0:

@@ -29,15 +29,15 @@ def tile_attend_teamcontrast_kernel(tc, query, keys_words, keys_scales, steep, u
     with ExitStack() as ctx:
         keep = ctx.enter_context(tc.tile_pool(name="keep", bufs=1))
         score_ps = ctx.enter_context(tc.psum_pool(name="score_ps", bufs=1))
-        turn_ps = ctx.enter_context(tc.psum_pool(name="turn_ps", bufs=4))
+        turn_ps = ctx.enter_context(tc.psum_pool(name="turn_ps", bufs=3))
 
         offsets = keep.tile([P, I // 16], U16, name="offsets")
-        nc.sync.dma_start(offsets[:], offs)
 
         key_scale_pool = keep.tile([P, T], U8, name="key_scale_pool", tag="kscale", align_bytes=64)
         nc.gpsimd.memset(key_scale_pool[:].bitcast(I32), 0)
         q_raw = keep.tile([P, PACK, Q], F32, name="q_raw")
         nc.sync.dma_start(q_raw[:], query.rearrange("(p j) q -> p j q", j=PACK))
+        nc.sync.dma_start(offsets[:], offs)
         for quad in range(4):
             nc.sync.dma_start(
                 key_scale_pool[32 * quad : 32 * quad + 4, :].bitcast(I32),
@@ -58,10 +58,6 @@ def tile_attend_teamcontrast_kernel(tc, query, keys_words, keys_scales, steep, u
         ident = keep.tile([P, P], F32, name="ident")
         make_identity(nc, ident[:])
 
-        warm = keep.tile([P, 1], F32, name="warm")
-        nc.vector.memset(warm[:], 0.0)
-        warmed = keep.tile([P, 1], F32, name="warmed")
-        nc.scalar.activation(warmed[:], warm[:], ACT.Sigmoid)
         q_bf = keep.tile([P, Q, PACK], BF16, name="q_bf", align_bytes=64)
         nc.scalar.copy(
             q_bf[:].rearrange("p (c i) t -> p c t i", i=4),
@@ -157,24 +153,8 @@ def tile_attend_teamcontrast_kernel(tc, query, keys_words, keys_scales, steep, u
 
         out_v = out.rearrange("(h p) e -> p h e", p=P)
 
-        def quantise(name, tag, v_bf, width):
-            v_codes = keep.tile([P, width], U32, name="codes" + name, tag=tag, align_bytes=64)
-            v_scales = keep.tile([P, width], U8, name="scales" + name, align_bytes=64)
-            nc.vector.quantize_mx(
-                out=v_codes[:].bitcast(FP8X4), scales=v_scales[:], in_=v_bf[:].rearrange("p e t -> p (e t)")
-            )
-            return v_codes, v_scales
-
-        def multiply(acc, h, operand):
-            nc.tensor.matmul_mx(
-                out=acc,
-                lhsT=early_codes[:, h * P : (h + 1) * P].bitcast(FP8X4),
-                lhsT_scale=early_scales[:, h * P : (h + 1) * P],
-                rhs=operand[0].bitcast(FP8X4),
-                rhs_scale=operand[1],
-                start=True,
-                stop=True,
-            )
+        def quantise(codes, scales, v_bf):
+            nc.vector.quantize_mx(out=codes.bitcast(FP8X4), scales=scales, in_=v_bf[:].rearrange("p e t -> p (e t)"))
 
         v2 = keep.tile([P, P, PACK], BF16, name="v2", align_bytes=64)
         v3 = keep.tile([P, P, PACK], BF16, name="v3", align_bytes=64)
@@ -184,29 +164,45 @@ def tile_attend_teamcontrast_kernel(tc, query, keys_words, keys_scales, steep, u
         turn(1, early_bf[:, Q + P : Q + 2 * P, :])
         gather(2)
         turn(2, v2[:])
-        early_codes, early_scales = quantise("_early", "val2", early_bf, Q + 2 * P)
-        op01 = (early_codes[:, Q : Q + 2 * P], early_scales[:, Q : Q + 2 * P])
-        acc01 = score_ps.tile([P, Q_HALVES, 2 * P], F32, name="acc01", tag="bank0")
-        for h in range(Q_HALVES):
-            multiply(acc01[:, h, :], h, op01)
-        res01 = keep.tile([P, Q_HALVES, 2 * P], F32, name="res01")
-        nc.scalar.copy(res01[:], acc01[:])
-        nc.sync.dma_start(out_v[:, :, 0 : 2 * P], res01[:])
         gather(3)
         turn(3, v3[:])
-        op2 = [t[:] for t in quantise("2", "val3", v2, P)]
-        acc2 = score_ps.tile([P, Q_HALVES, P], F32, name="acc2", tag="bank1")
+        codes = keep.tile([P, Q + E], U32, name="codes", tag="val3", align_bytes=64)
+        scales = keep.tile([P, Q + E], U8, name="scales", align_bytes=64)
+        quantise(codes[:, 0 : Q + 2 * P], scales[:, 0 : Q + 2 * P], early_bf)
+        quantise(codes[:, Q + 2 * P : Q + 3 * P], scales[:, Q + 2 * P : Q + 3 * P], v2)
+        quantise(codes[:, Q + 3 * P : Q + E], scales[:, Q + 3 * P : Q + E], v3)
+
+        def multiply(acc, h, e0, e1):
+            nc.tensor.matmul_mx(
+                out=acc,
+                lhsT=codes[:, h * P : (h + 1) * P].bitcast(FP8X4),
+                lhsT_scale=scales[:, h * P : (h + 1) * P],
+                rhs=codes[:, Q + e0 : Q + e1].bitcast(FP8X4),
+                rhs_scale=scales[:, Q + e0 : Q + e1],
+                start=True,
+                stop=True,
+            )
+
         for h in range(Q_HALVES):
-            multiply(acc2[:, h, :], h, op2)
+            acc = score_ps.tile([P, 2 * P], F32, name="acc01_%d" % h, tag="bank%d" % h)
+            multiply(acc[:], h, 0, 2 * P)
+            res = keep.tile([P, 2 * P], F32, name="res01_%d" % h)
+            if h == 0:
+                nc.scalar.copy(res[:], acc[:])
+            else:
+                nc.vector.tensor_copy(res[:], acc[:])
+            nc.sync.dma_start(out_v[:, h, 0 : 2 * P], res[:])
+        acc2 = score_ps.tile([P, Q_HALVES, P], F32, name="acc2", tag="bank4")
+        for h in range(Q_HALVES):
+            multiply(acc2[:, h, :], h, 2 * P, 3 * P)
         res2 = keep.tile([P, Q_HALVES, P], F32, name="res2")
-        nc.vector.tensor_copy(res2[:], acc2[:])
+        nc.scalar.copy(res2[:], acc2[:])
         nc.sync.dma_start(out_v[:, :, 2 * P : 3 * P], res2[:])
-        op3 = [t[:] for t in quantise("3", "codes3", v3, P)]
         for h in range(Q_HALVES):
             acc3 = score_ps.tile([P, P], F32, name="acc3_%d" % h, tag="bank%d" % (2 + h))
-            multiply(acc3[:], h, op3)
+            multiply(acc3[:], h, 3 * P, E)
             res3 = keep.tile([P, P], F32, name="res3_%d" % h)
-            if h == 0:
+            if h == 1:
                 nc.scalar.copy(res3[:], acc3[:])
                 nc.scalar.dma_start(out_v[:, h, 3 * P : E], res3[:])
             else:

from contextlib import ExitStack

import concourse.mybir as mybir
from concourse.masks import make_identity

D, T, I, Q, E = 512, 2048, 512, 256, 512
TEAM = 8
FLOPS = 2 * D * I * Q + 2 * I * Q * E

F32 = mybir.dt.float32
BF16 = mybir.dt.bfloat16
I32 = mybir.dt.int32
U32 = mybir.dt.uint32
U16 = mybir.dt.uint16
U8 = mybir.dt.uint8
FP8X4 = mybir.dt.float8_e4m3fn_x4
ACT = mybir.ActivationFunctionType
ALU = mybir.AluOpType
AXIS = mybir.AxisListType

P = 128
PACK = 4
E_BLOCKS = E // P
Q_HALVES = Q // P


def tile_attend_teamcontrast_kernel(tc, query, keys_words, keys_scales, steep, us, vals, offs, out):
    nc = tc.nc
    with ExitStack() as ctx:
        keep = ctx.enter_context(tc.tile_pool(name="keep", bufs=1))
        score_ps = ctx.enter_context(tc.psum_pool(name="score_ps", bufs=1))
        turn_ps = ctx.enter_context(tc.psum_pool(name="turn_ps", bufs=3))

        offsets = keep.tile([P, I // 16], U16, name="offsets")

        key_scale_pool = keep.tile([P, T], U8, name="key_scale_pool", tag="kscale", align_bytes=64)
        nc.gpsimd.memset(key_scale_pool[:].bitcast(I32), 0)
        q_raw = keep.tile([P, PACK, Q], F32, name="q_raw")
        nc.sync.dma_start(q_raw[:], query.rearrange("(p j) q -> p j q", j=PACK))
        nc.sync.dma_start(offsets[:], offs)
        for quad in range(4):
            nc.sync.dma_start(
                key_scale_pool[32 * quad : 32 * quad + 4, :].bitcast(I32),
                keys_scales[0, 4 * quad : 4 * quad + 4, :].bitcast(I32),
            )
        key_word_pool = keep.tile([P, T], I32, name="key_word_pool", align_bytes=64)
        nc.sync.dma_start(key_word_pool[:], keys_words[0].rearrange("p n t -> p (n t)").bitcast(I32))
        steep_sb = keep.tile([P, PACK], F32, name="steep_sb")
        nc.sync.dma_start(steep_sb[:], steep.rearrange("(p r) o -> p (r o)", r=PACK))
        us_sb = keep.tile([P, PACK], F32, name="us_sb")
        nc.sync.dma_start(us_sb[:], us.rearrange("(p r) o -> p (r o)", r=PACK))
        val_pool = []
        for b in range(E_BLOCKS):
            t = keep.tile([P, T], F32, name="val_pool%d" % b, tag="val%d" % b, align_bytes=64)
            nc.sync.dma_start(t[:], vals[b * P : (b + 1) * P, :])
            val_pool.append(t)

        ident = keep.tile([P, P], F32, name="ident")
        make_identity(nc, ident[:])

        q_bf = keep.tile([P, Q, PACK], BF16, name="q_bf", align_bytes=64)
        nc.scalar.copy(
            q_bf[:].rearrange("p (c i) t -> p c t i", i=4),
            q_raw[:].rearrange("p t (c i) -> p c t i", i=4),
        )
        ks_list = keep.tile([P, I], U8, name="ks_list", align_bytes=64)
        nc.vector.tensor_copy(ks_list[:], key_scale_pool[:].indirect(offsets[:]))
        k_scales = keep.tile([P, PACK, P], U8, name="k_scales", align_bytes=64)
        nc.vector.tensor_copy(k_scales[:], ks_list[:].rearrange("p (s r) -> p r s", r=PACK))
        q_codes = keep.tile([P, Q], U32, name="q_codes", tag="kscale", align_bytes=64)
        q_scales = keep.tile([P, Q], U8, name="q_scales", align_bytes=64)
        nc.vector.quantize_mx(
            out=q_codes[:].bitcast(FP8X4), scales=q_scales[:], in_=q_bf[:].rearrange("p q t -> p (q t)")
        )
        k_codes = keep.tile([P, PACK, P], U32, name="k_codes", align_bytes=64)
        nc.vector.tensor_copy(
            k_codes[:].rearrange("p r s -> p s r"), key_word_pool[:].bitcast(U32).indirect(offsets[:])
        )

        teams = Q // TEAM
        scores, sums, diffs = [], [], []
        for r in range(PACK):
            bank = score_ps.tile([P, Q], F32, name="scores%d" % r, tag="bank%d" % r)
            nc.tensor.matmul_mx(
                out=bank[:],
                lhsT=k_codes[:, r, :].bitcast(FP8X4),
                lhsT_scale=k_scales[:, r, :],
                rhs=q_codes[:].bitcast(FP8X4),
                rhs_scale=q_scales[:],
                start=True,
                stop=True,
            )
            scores.append(bank[:].rearrange("p (g j) -> p g j", j=TEAM))

        def team_sum(r):
            s = keep.tile([P, teams], F32, name="team_sum%d" % r, tag="slot%d" % ((r + 2) % 4), align_bytes=64)
            nc.vector.tensor_reduce(s[:], scores[r], AXIS.X, ALU.add)
            sums.append(s)

        def contrast(r):
            d = keep.tile([P, teams, TEAM], F32, name="diff%d" % r, align_bytes=64)
            nc.vector.scalar_tensor_tensor(
                d[:],
                sums[r][:].unsqueeze(2).to_broadcast([P, teams, TEAM]),
                -1.0 / TEAM,
                scores[r],
                ALU.mult,
                ALU.add,
            )
            diffs.append(d)

        team_sum(0)
        for r in range(PACK):
            if r + 1 < PACK:
                team_sum(r + 1)
            contrast(r)

        w_planes = keep.tile([P, PACK, Q], BF16, name="w_planes", align_bytes=64)
        gates = []

        def gate(r):
            g = keep.tile([P, Q], F32, name="gate%d" % r)
            nc.scalar.activation(
                g[:], diffs[r][:].rearrange("p g j -> p (g j)"), ACT.Sigmoid, scale=steep_sb[:, r : r + 1]
            )
            gates.append(g)

        gate(0)
        for r in range(PACK):
            if r + 1 < PACK:
                gate(r + 1)
            nc.scalar.activation(w_planes[:, r, :], gates[r][:], ACT.Copy, scale=us_sb[:, r : r + 1])

        early_bf = keep.tile([P, Q + 2 * P, PACK], BF16, name="early_bf", align_bytes=64)
        nc.scalar.copy(
            early_bf[:, 0:Q, :].rearrange("p (c i) t -> p c t i", i=4),
            w_planes[:].rearrange("p t (c i) -> p c t i", i=4),
        )

        picked = {}

        def gather(b):
            g = keep.tile([P, I], BF16, name="picked%d" % b, tag="slot%d" % b, align_bytes=64)
            nc.vector.tensor_copy(g[:], val_pool[b][:].indirect(offsets[:]))
            picked[b] = g

        def turn(b, v_bf):
            words = picked[b][:].bitcast(F32)
            xt = turn_ps.tile([P, 2, P], F32, name="xt")
            for u in range(2):
                nc.tensor.transpose(xt[:, u, :], words[:, u : I // 2 : 2], ident[:])
            nc.scalar.copy(v_bf.bitcast(F32), xt[:].rearrange("p u e -> p e u"))

        out_v = out.rearrange("(h p) e -> p h e", p=P)

        def quantise(codes, scales, v_bf):
            nc.vector.quantize_mx(out=codes.bitcast(FP8X4), scales=scales, in_=v_bf[:].rearrange("p e t -> p (e t)"))

        v2 = keep.tile([P, P, PACK], BF16, name="v2", align_bytes=64)
        v3 = keep.tile([P, P, PACK], BF16, name="v3", align_bytes=64)
        gather(0)
        turn(0, early_bf[:, Q : Q + P, :])
        gather(1)
        turn(1, early_bf[:, Q + P : Q + 2 * P, :])
        gather(2)
        turn(2, v2[:])
        gather(3)
        turn(3, v3[:])
        codes = keep.tile([P, Q + E], U32, name="codes", tag="val3", align_bytes=64)
        scales = keep.tile([P, Q + E], U8, name="scales", align_bytes=64)
        quantise(codes[:, 0 : Q + 2 * P], scales[:, 0 : Q + 2 * P], early_bf)
        quantise(codes[:, Q + 2 * P : Q + 3 * P], scales[:, Q + 2 * P : Q + 3 * P], v2)
        quantise(codes[:, Q + 3 * P : Q + E], scales[:, Q + 3 * P : Q + E], v3)

        def multiply(acc, h, e0, e1):
            nc.tensor.matmul_mx(
                out=acc,
                lhsT=codes[:, h * P : (h + 1) * P].bitcast(FP8X4),
                lhsT_scale=scales[:, h * P : (h + 1) * P],
                rhs=codes[:, Q + e0 : Q + e1].bitcast(FP8X4),
                rhs_scale=scales[:, Q + e0 : Q + e1],
                start=True,
                stop=True,
            )

        for h in range(Q_HALVES):
            acc = score_ps.tile([P, 2 * P], F32, name="acc01_%d" % h, tag="bank%d" % h)
            multiply(acc[:], h, 0, 2 * P)
            res = keep.tile([P, 2 * P], F32, name="res01_%d" % h)
            if h == 0:
                nc.scalar.copy(res[:], acc[:])
            else:
                nc.vector.tensor_copy(res[:], acc[:])
            nc.sync.dma_start(out_v[:, h, 0 : 2 * P], res[:])
        acc2 = score_ps.tile([P, Q_HALVES, P], F32, name="acc2", tag="bank4")
        for h in range(Q_HALVES):
            multiply(acc2[:, h, :], h, 2 * P, 3 * P)
        res2 = keep.tile([P, Q_HALVES, P], F32, name="res2")
        nc.scalar.copy(res2[:], acc2[:])
        nc.sync.dma_start(out_v[:, :, 2 * P : 3 * P], res2[:])
        for h in range(Q_HALVES):
            acc3 = score_ps.tile([P, P], F32, name="acc3_%d" % h, tag="bank%d" % (2 + h))
            multiply(acc3[:], h, 3 * P, E)
            res3 = keep.tile([P, P], F32, name="res3_%d" % h)
            if h == 1:
                nc.scalar.copy(res3[:], acc3[:])
                nc.scalar.dma_start(out_v[:, h, 3 * P : E], res3[:])
            else:
                nc.vector.tensor_copy(res3[:], acc3[:])
                nc.sync.dma_start(out_v[:, h, 3 * P : E], res3[:])
